import numpy as np, ml_dtypes
CORES = [12,28,60,100,156,228]
N = 6
import mx_ref
NC, GR, GC, T = 256, 3, 2, 6
TA, TB = T // GC, T // GR
BF = ml_dtypes.bfloat16
def setup_inputs(rng):
    def f(*shape):
        return mx_ref.flush((rng.standard_normal(shape, dtype=np.float32) * np.exp2(rng.integers(-2, 3, shape[:-1] + (1,)))).astype(BF))
    return {"a": f(N, 128, TA * 512), "b": f(N, 128, TB * 4 * NC)}
def setup_inputs_blocks(rng):
    d = setup_inputs(rng)
    for k in ("a", "b"): d[k] = mx_ref.spread(d[k], rng, 2)
    return d
def setup_inputs_wide(rng):
    d = setup_inputs(rng)
    for k in ("a", "b"): d[k] = mx_ref.flush((d[k].astype(np.float32) * np.exp2(rng.integers(-8, 9, (N, 1, 1))).astype(np.float32)).astype(BF))
    return d
def setup_inputs_zeros(rng):
    d = setup_inputs(rng); v = d["b"].reshape(N, 128, -1, 4).copy()
    v[np.broadcast_to((rng.random((N, 1, v.shape[2], 1)) < 0.33), v.shape)] = 0
    d["b"] = v.reshape(d["b"].shape)
    return d
def reference(a, b):
    A = lambda i, s: mx_ref.quantize(a[i * GC + s // TA][:, 512 * (s % TA):512 * (s % TA) + 512])
    B = lambda s, j: mx_ref.quantize(b[(s // TB) * GC + j][:, 4 * NC * (s % TB):4 * NC * (s % TB) + 4 * NC])
    y = np.zeros((N, 128, NC), np.float32)
    for r in range(N):
        for s in range(T):
            p = mx_ref.matmul(A(r // GC, s), B(s, r % GC))
            y[r] = p if s == 0 else y[r] + p
    return {"y": y}

from concourse.bass import DstId, RemoteDMATransfer
from concourse.mybir import dt

WORLD = 256
GR, GC, NS = 3, 2, 6
TA, TB = NS // GC, NS // GR
W = {"a": 128, "b": 256}
NT = {"a": TA, "b": TB}

SCRATCH = {
    "xa": ("sbuf", [128, TA * 4 * W["a"]], "bfloat16"),
    "xb": ("sbuf", [128, TB * 4 * W["b"]], "bfloat16"),
    "qa": ("sbuf", [128, NS * W["a"]], "float8_e4m3fn_x4"),
    "sa": ("sbuf", [128, NS * W["a"]], "uint8"),
    "qb": ("sbuf", [128, NS * W["b"]], "float8_e4m3fn_x4"),
    "sb": ("sbuf", [128, NS * W["b"]], "uint8"),
    "acc": ("psum", [128, 512], "float32"),
    "out": ("sbuf", [128, W["b"]], "float32"),
}

UNITS = {"a": ("a", 0, 384), "a01": ("a", 0, 256), "a2": ("a", 256, 384), "b": ("b", 0, 512), "b0": ("b", 0, 256), "b1": ("b", 256, 512)}
PIECES = {}
for _u, (_t, _lo, _hi) in UNITS.items():
    PIECES[_u + "c"] = (_t, True, _lo, _hi, _u)
    PIECES[_u + "s"] = (_t, False, _lo, _hi, _u)

_RELAY_B = [[("b0c", "f0", "all", "lo")], [("b1c", "n0", "all", "hi")], [("bs", "f1", "all", "all")]]
CFG = {
    "loads": {"*": ["b0", "b1", "a"]},
    "sends": {
        "*": _RELAY_B + [[("ac", "n1", "all", "all")], [("as", "f1", "all", "all")]],
        "SSS": _RELAY_B + [[("ac", "D", "all", "lo")], [("as", "D", "all", "lo")]],
        "SXX": _RELAY_B + [[("ac", "D", "all", "lo")], [("as", "D", "all", "lo")]],
    },
}


def _sem_names(cfg):
    names = ["sent", "mm", "cp", "st"]
    us, ps = [], []
    for l in cfg["loads"].values():
        us += [u for u in l if u not in us]
    for calls in cfg["sends"].values():
        for call in calls:
            ps += [e[0] for e in call if e[0] not in ps]
    names += ["ld_" + u for u in us] + ["q_" + u for u in us] + ["h_" + p for p in ps]
    for p in ps:
        t, lab = PIECES[p][0], PIECES[p][4]
        for k in range(GC if t == "a" else GR):
            if "r%d_%s" % (k, lab) not in names:
                names.append("r%d_%s" % (k, lab))
    return names


SEMAPHORES = _sem_names(CFG)


def _bits(m):
    return [k for k in range(m.bit_length()) if (m >> k) & 1]


def _mask(bits):
    m = 0
    for k in bits:
        m |= 1 << k
    return m


def _view(T, t, codes, lo, hi):
    if codes:
        return T["q" + t][:, lo:hi].bitcast(dt.uint8)
    return T["s" + t][:, lo:hi]


def _cls(T, topo, r):
    cores = list(T.cores)
    i, j = r // GC, r % GC
    c = cores[r]
    da = [cores[i * GC + (1 - j)]]
    db = [cores[((i + k) % GR) * GC + j] for k in range(1, GR)]
    key = "".join("S" if topo.may_write(c, d) else "X" for d in da) + "".join(sorted("S" if topo.may_write(c, d) else "X" for d in db))
    return key, da, db


def _pick(table, key):
    return table[key] if key in table else table["*"]


def build(T, topo, cfg):
    cores = list(T.cores)
    calls = {c: [] for c in cores}
    fwd = {}
    lands = {c: [] for c in cores}
    for r, c in enumerate(cores):
        i, j = r // GC, r % GC
        key, da, db = _cls(T, topo, r)
        chip = [x for x in range(WORLD) if x != c and topo.host(x) == topo.host(c) and topo.chip(x) == topo.chip(c)]
        mate = [x for x in range(WORLD) if topo.mates(c, x)][0]
        own = [x for x in chip if topo.may_write(x, mate)]
        H = {}
        for hk, lst in (("n", [x for x in own if topo.die(x) == topo.die(c)]), ("f", [x for x in own if topo.die(x) != topo.die(c)])):
            for k, x in enumerate(lst):
                H[hk + str(k)] = x
        loads = _pick(cfg["loads"], key)
        for pos, call in enumerate(_pick(cfg["sends"], key)):
            trs, need = [], []
            for piece, route, sel, group in call:
                t, codes, lo, hi, lab = PIECES[piece]
                base = (j * TA if t == "a" else i * TB) * W[t]
                dsts = [d for d in (da if t == "a" else db) if sel == "all" or (sel == "s") == topo.may_write(c, d)]
                if not dsts:
                    continue
                rsem = "r%d_%s" % (j if t == "a" else i, lab)
                need += [u for u in loads if UNITS[u][0] == t and UNITS[u][1] < hi and UNITS[u][2] > lo and u not in need]
                if route == "D":
                    m = topo.mask(c, dsts[0])
                    trs.append((t, codes, base + lo, base + hi, dsts, rsem, m))
                    eta = pos
                else:
                    h = H[route]
                    m = topo.mask(h, dsts[0])
                    on, off = _bits(topo.mask(c, h)), _bits(m)
                    eng = {"all": on, "lo": [k for k in on if k in off], "hi": [k for k in on if k not in off]}[group]
                    trs.append((t, codes, base + lo, base + hi, [h], "h_" + piece, _mask(eng)))
                    fwd.setdefault(h, []).append(("h_" + piece, len(eng), [(t, codes, base + lo, base + hi, dsts, rsem, m)]))
                    eta = pos + 6
                for d in dsts:
                    lands[d].append((t, base + lo, base + hi, rsem, len(_bits(m)), eta))
            if trs:
                calls[c].append((need, trs))
    return calls, fwd, lands


def _issue(g, T, topo, core, transfers):
    trs, n = [], 0
    for t, codes, lo, hi, dsts, sem, m in transfers:
        ids = []
        for d in dsts:
            rid, pid = topo.addr(d, core)
            ids.append(DstId(rid=rid, pnc=pid))
        trs.append(RemoteDMATransfer(dst_ids=ids, dma_engine_mask=m, remote_sem=T.sem[sem], srcs=[_view(T, t, codes, lo, hi)],
                                     dsts=[_view(T, t, codes, lo, hi) for _ in dsts]))
        n += len(_bits(m))
    g.remote_dma_fused(trs, local_sem=T.sem.sent)
    return n


def rank_program(g, core, T, topo):
    cfg = CFG
    calls, fwd, lands = build(T, topo, cfg)
    rank = T.rank_of(core)
    if rank is None:
        if core in fwd:
            sent = 0
            for sem, cnt, transfers in fwd[core]:
                g.wait_ge(T.sem[sem], cnt)
                sent += _issue(g, T, topo, core, transfers)
            g.wait_ge(T.sem.sent, sent)
        return
    i, j = rank // GC, rank % GC
    loads = _pick(cfg["loads"], _cls(T, topo, rank)[0])
    own = {"a": j * TA, "b": i * TB}
    for u in loads:
        t, lo, hi = UNITS[u]
        g.sync.dma_start(T["x" + t][:, 4 * lo:4 * hi], T[t][:, 4 * lo:4 * hi]).then_inc(T.sem["ld_" + u], 16)
    for u in loads:
        t, lo, hi = UNITS[u]
        base = own[t] * W[t]
        g.vector.wait_ge(T.sem["ld_" + u], 16)
        g.vector.quantize_mx(T["q" + t][:, base + lo:base + hi], T["s" + t][:, base + lo:base + hi],
                             T["x" + t][:, 4 * lo:4 * hi]).then_inc(T.sem["q_" + u], 1)
    sent, waited = 0, []
    for need, transfers in calls[core]:
        for u in need:
            if u not in waited:
                g.wait_ge(T.sem["q_" + u], 1)
                waited.append(u)
        sent += _issue(g, T, topo, core, transfers)
    tot, eta = {}, {}
    for t, lo, hi, sem, n, e in lands[core]:
        tot[sem] = tot.get(sem, 0) + n
        eta[sem] = max(eta.get(sem, 0), e)

    def needs(s):
        out = []
        for t in ("a", "b"):
            lo, hi = s * W[t], (s + 1) * W[t]
            if own[t] <= s < own[t] + NT[t]:
                b = own[t] * W[t]
                out += [("q_" + u, 1, loads.index(u) - 100) for u in loads if UNITS[u][0] == t and UNITS[u][1] + b < hi and UNITS[u][2] + b > lo]
            else:
                for t2, l2, h2, sem, n, e in lands[core]:
                    if t2 == t and l2 < hi and h2 > lo and sem not in [x[0] for x in out]:
                        out.append((sem, tot[sem], eta[sem]))
        return out

    slices = sorted(range(NS), key=lambda s: (max(x[2] for x in needs(s)), s))
    done = []
    for k, s in enumerate(slices):
        for sem, n, _e in needs(s):
            if sem not in done:
                g.tensor.wait_ge(T.sem[sem], n)
                done.append(sem)
        mmi = g.tensor.matmul_mx(T.acc[:, 0:W["b"]], T.qa[:, s * W["a"]:(s + 1) * W["a"]], T.sa[:, s * W["a"]:(s + 1) * W["a"]],
                                 T.qb[:, s * W["b"]:(s + 1) * W["b"]], T.sb[:, s * W["b"]:(s + 1) * W["b"]], k == 0, k == NS - 1)
    mmi.then_inc(T.sem.mm, 1)
    g.vector.wait_ge(T.sem.mm, 1)
    g.vector.tensor_copy(T.out[:], T.acc[:, 0:W["b"]]).then_inc(T.sem.cp, 1)
    g.sync.wait_ge(T.sem.cp, 1)
    g.sync.dma_start(T.y[:], T.out[:]).then_inc(T.sem.st, 16)
    g.sync.wait_ge(T.sem.st, 16)
    g.wait_ge(T.sem.sent, sent)
